import numpy as np
import ml_dtypes


def mxq(x, axis, fmt="e4m3"):
    dtype, down = {"e4m3": (ml_dtypes.float8_e4m3fn, 7), "e5m2": (ml_dtypes.float8_e5m2, 14)}[fmt]
    v = np.moveaxis(np.asarray(x, np.float32).astype(ml_dtypes.bfloat16).astype(np.float64), axis, -1)
    blocks = v.reshape(v.shape[:-1] + (-1, 32))
    amax = np.abs(blocks).max(-1, keepdims=True)
    byte = np.maximum(np.where(amax > 0, np.frexp(amax)[1] - 1 + 127, 0) - down, 1)
    scale = np.exp2(byte - 127.0)
    codes = (blocks / scale).astype(np.float32).astype(dtype).astype(np.float64)
    return np.moveaxis((codes * scale).reshape(v.shape), -1, axis)


WIDE = False


def mx_kscale(k):
    if not WIDE:
        return np.ones(k)
    levels = np.array([10, -10, 5, -5, 0])
    if k % 512:
        return np.exp2(np.random.permutation(np.resize(levels, k // 32))).repeat(32)
    a = np.empty((k // 512, 16))
    for p in range(k // 512):
        a[p, :8] = np.random.permutation(np.resize(levels, 8))
        for g in range(8):
            far = levels[np.abs(levels - a[p, g]) >= 10]
            a[p, g + 8] = far[np.random.randint(len(far))]
    return np.exp2(a.ravel()).repeat(32)


def f64(x):
    return np.asarray(x).astype(np.float64)


def striped(idx):
    return np.tile(idx.reshape(-1, 16).T, (8, 1)).astype(np.uint16)


def unstriped(offs):
    return offs[:16].T.reshape(-1).astype(np.int64)


def pack_weight(w):
    k, n = w.shape
    w = f64(np.asarray(w, np.float32).astype(ml_dtypes.bfloat16)).reshape(k // 32, 32, n)
    amax = np.abs(w).max(1)
    byte = np.clip(np.where(amax > 0, np.frexp(amax)[1] - 1 + 127 - 7, 1), 1, 254)
    scaled = (w * np.exp2(127.0 - byte)[:, None, :]).reshape(k, n).astype(np.float32)
    words = np.ascontiguousarray(scaled.reshape(k // 512, 128, 4, n).transpose(0, 1, 3, 2)).astype(ml_dtypes.float8_e4m3fn).view(np.uint8)
    return words, np.ascontiguousarray(byte.astype(np.uint8).reshape(k // 512, 16, n))


def unpack_weight(words, scales):
    g, p, n, _ = words.shape
    vals = np.ascontiguousarray(words).view(ml_dtypes.float8_e4m3fn).astype(np.float64) * np.repeat(np.exp2(scales.astype(np.float64) - 127.0), 8, axis=1)[..., None]
    return vals.transpose(0, 1, 3, 2).reshape(g * 512, n)


K, T, S, H, Z, W = 512, 1024, 512, 512, 512, 2048


def setup_inputs():
    n = np.random.standard_normal
    s = mx_kscale(K)[:, None]
    u = mx_kscale(H)
    packed_xT = pack_weight(n((K, T)) * s)
    packed_eT = pack_weight(n((K, W)) * s)
    return {
        "x_words": packed_xT[0],
        "x_scales": packed_xT[1],
        "w1": (n((K, H)) / np.sqrt(K) / s).astype(np.float32),
        "e_words": packed_eT[0],
        "e_scales": packed_eT[1],
        "w2": (n((K, H)) / np.sqrt(K) / s).astype(np.float32),
        "unit": (np.random.uniform(0.6, 1.4, (H, 1)) * u[:, None]).astype(np.float32),
        "unit2": (np.random.uniform(0.6, 1.4, (H, 1)) / np.sqrt(H) / u[:, None]).astype(np.float32),
        "offs": striped(np.random.permutation(T)[:S]),
        "rgt": striped(np.random.permutation(W)[:Z]),
        "ln": striped(np.random.permutation(S)),
        "rn": striped(np.random.permutation(Z)),
        "dsp": striped(np.random.permutation(Z)),
    }


def reference(x_words, x_scales, w1, e_words, e_scales, w2, unit, unit2, offs, rgt, ln, rn, dsp):
    xq = unpack_weight(x_words, x_scales)[:, unstriped(offs)]
    y = mxq(f64(w1), 0, "e4m3").T @ xq
    yl = y[:, unstriped(ln)]
    edl = y - (0.6 * yl)
    hid = f64(unit) * edl
    e_rgt = unpack_weight(e_words, e_scales)[:, unstriped(rgt)]
    ye = mxq(f64(w2), 0, "e4m3").T @ e_rgt
    yr = ye[:, unstriped(rn)]
    edr = ye - (0.6 * yr)
    hid2 = f64(unit2) * edr
    sc = mxq(hid, 0, "e4m3").T @ mxq(hid2, 0, "e4m3")
    sshift = sc[:, unstriped(dsp)]
    return np.maximum(sc, 0.8 * sshift)

@@ -1,0 +1,198 @@
+from contextlib import ExitStack
+
+import concourse.mybir as mybir
+
+F32 = mybir.dt.float32
+BF16 = mybir.dt.bfloat16
+I32 = mybir.dt.int32
+U32 = mybir.dt.uint32
+U16 = mybir.dt.uint16
+U8 = mybir.dt.uint8
+FP8X4 = mybir.dt.float8_e4m3fn_x4
+COPY = mybir.ActivationFunctionType.Copy
+ALU = mybir.AluOpType
+
+P = 128
+PACK = 4
+N = 512
+T_LEFT, T_RIGHT = 1024, 2048
+HALF = N // 2
+FLOPS = 3 * 2 * N * N * N
+
+
+def tile_picked_ystrmat_max_p_kernel(
+    tc, x_words, x_scales, w1, e_words, e_scales, w2, unit, unit2, offs, rgt, ln, rn, dsp, out
+):
+    nc = tc.nc
+    with ExitStack() as ctx:
+        sb = ctx.enter_context(tc.tile_pool(name="sb", bufs=1))
+        ps = ctx.enter_context(tc.psum_pool(name="ps", bufs=1))
+
+        def load_list(name, src):
+            t = sb.tile([P, N // 16], U16, name=name)
+            nc.sync.dma_start(t[:], src)
+            return t
+
+        def load_words(name, src, width):
+            t = sb.tile([P, width], U32, name=name, tag=name, align_bytes=64)
+            nc.sync.dma_start(out=t[:].bitcast(I32), in_=src[0].rearrange("p n t -> p (n t)").bitcast(I32))
+            return t
+
+        def load_scales(name, src, width, queue):
+            t = sb.tile([P, width], U8, name=name, align_bytes=64)
+            nc.gpsimd.memset(t[:].bitcast(I32), 0)
+            for q in range(4):
+                queue.dma_start(out=t[32 * q : 32 * q + 4, :].bitcast(I32), in_=src[0, 4 * q : 4 * q + 4, :].bitcast(I32))
+            return t
+
+        def load_scales_spread(name, src, width):
+            t = sb.tile([P, width], U8, name=name, align_bytes=64)
+            for q in range(4):
+                rows = src[0, 4 * q : 4 * q + 4, :].bitcast(I32)
+                nc.sync.dma_start(out=t[32 * q : 32 * q + 32, :].bitcast(I32), in_=rows.partition_broadcast(8))
+            return t
+
+        def load_weight_half(name, src, h):
+            t = sb.tile([P, PACK, HALF], F32, name=name)
+            nc.sync.dma_start(out=t[:], in_=src.rearrange("(p j) c -> p j c", j=PACK)[:, :, h * HALF : (h + 1) * HALF])
+            return t
+
+        def load_unit(name, src):
+            t = sb.tile([P, PACK], F32, name=name, tag=name, align_bytes=64)
+            nc.gpsimd.dma_start(out=t[:], in_=src.rearrange("(p t) o -> p (t o)", t=PACK))
+            return t
+
+        def pick(name, table, lst, dtype, tag):
+            t = sb.tile([P, N], dtype, name=name, tag=tag, align_bytes=64)
+            nc.vector.tensor_copy(t[:], table[:].indirect(lst[:]))
+            return t
+
+        def cast_weight(wb, raw, h, lo, hi, on_scalar):
+            dst = wb[:, :, h * 64 + lo : h * 64 + hi, :].rearrange("p t m j -> p m j t")
+            src = raw[:, :, PACK * lo : PACK * hi].rearrange("p j (m t) -> p m j t", t=PACK)
+            if on_scalar:
+                nc.scalar.copy(out=dst, in_=src)
+            else:
+                nc.vector.tensor_copy(out=dst, in_=src)
+
+        def quantize(codes, scales, grouped, lo, hi):
+            nc.vector.quantize_mx(out=codes[:, lo:hi].bitcast(FP8X4), scales=scales[:, lo:hi], in_=grouped)
+
+        def mx_tiles(name):
+            codes = sb.tile([P, N], U32, name=name + "_codes", align_bytes=64)
+            scales = sb.tile([P, N], U8, name=name + "_scales", align_bytes=64)
+            return codes, scales
+
+        def product(bank, lhs, cols, rhs):
+            acc = ps.tile([P, N], F32, name="acc", tag="bank%d" % bank)
+            nc.tensor.matmul_mx(
+                out=acc[:], lhsT=lhs[0][:, cols].bitcast(FP8X4), lhsT_scale=lhs[1][:, cols],
+                rhs=rhs[0][:].bitcast(FP8X4), rhs_scale=rhs[1][:], start=True, stop=True)
+            return acc
+
+        def scaled_out(dst, acc, factor, on_scalar):
+            if on_scalar:
+                nc.scalar.activation(dst, acc[:], COPY, scale=factor)
+            else:
+                nc.vector.tensor_scalar(out=dst, in0=acc[:], scalar1=factor, scalar2=None, op0=ALU.mult)
+
+        def neighbours(share, planes, t, lst, lo, hi):
+            nc.scalar.activation(share[:, t, lo:hi], planes[:, t, :].indirect(lst[:, lo // 16 : hi // 16]), COPY, scale=-0.6)
+
+        def combine(grouped, planes, share, lo, hi):
+            dst = grouped.rearrange("p (c i t) -> p c t i", i=4, t=PACK)
+            a = planes[:, :, lo:hi].rearrange("p t (c i) -> p c t i", i=4)
+            b = share[:, :, lo:hi].rearrange("p t (c i) -> p c t i", i=4)
+            nc.vector.tensor_tensor(out=dst, in0=a, in1=b, op=ALU.add)
+
+        offs_t = load_list("offs_t", offs)
+        xw = load_words("xw", x_words, T_LEFT)
+        xs = load_scales_spread("xs", x_scales, T_LEFT)
+        w1_raw = [load_weight_half("w1_raw%d" % h, w1, h) for h in range(2)]
+        u1 = load_unit("u1", unit)
+        u2 = load_unit("u2", unit2)
+        rgt_t = load_list("rgt_t", rgt)
+        ln_t = load_list("ln_t", ln)
+        es = load_scales_spread("es", e_scales, T_RIGHT)
+        ew = load_words("ew", e_words, T_RIGHT)
+        w2_raw = [load_weight_half("w2_raw%d" % h, w2, h) for h in range(2)]
+        rn_t = load_list("rn_t", rn)
+        dsp_t = load_list("dsp_t", dsp)
+
+        xq = (pick("xq_w", xw, offs_t, U32, "xq_w"), pick("xq_s", xs, offs_t, U8, "xq_s"))
+        w1b = sb.tile([P, PACK, P, PACK], BF16, name="w1b", align_bytes=64)
+        cast_weight(w1b, w1_raw[0], 0, 0, 64, True)
+        cast_weight(w1b, w1_raw[1], 1, 0, 44, False)
+        cast_weight(w1b, w1_raw[1], 1, 44, 64, True)
+        w1q = mx_tiles("w1q")
+        w1flat = w1b[:].rearrange("p t m j -> p (t m j)")
+        y_pad = sb.tile([P, (PACK + 1) * N], F32, name="y_pad")
+        nc.gpsimd.memset(y_pad[:, PACK * N :], 0.0)
+        y = y_pad[:, : PACK * N].rearrange("p (t n) -> p t n", t=PACK)
+        yl = sb.tile([P, PACK, N], F32, name="yl")
+        for t in reversed(range(PACK)):
+            quantize(w1q[0], w1q[1], w1flat[:, t * N : (t + 1) * N], t * P, (t + 1) * P)
+        for t in reversed(range(PACK)):
+            acc = product(t, w1q, slice(t * P, (t + 1) * P), xq)
+            scaled_out(y[:, t, :], acc, u1[:, t : t + 1], t == PACK - 1)
+        for t in reversed(range(PACK)):
+            nc.scalar.activation(yl[:, t, :], y_pad[:, t * N : (t + 2) * N].indirect(ln_t[:]), COPY, scale=-0.6)
+
+        eq = (pick("eq_w", ew, rgt_t, U32, "u1"), pick("eq_s", es, rgt_t, U8, "eq_s"))
+        w2b = sb.tile([P, PACK, P, PACK], BF16, name="w2b", tag="ew", align_bytes=64)
+        for h in range(2):
+            cast_weight(w2b, w2_raw[h], h, 0, 64, False)
+        w2q = mx_tiles("w2q")
+        w2flat = w2b[:].rearrange("p t m j -> p (t m j)")
+        ye = sb.tile([P, PACK, N], F32, name="ye")
+        yr = sb.tile([P, PACK, N], F32, name="yr")
+        for t in range(PACK):
+            quantize(w2q[0], w2q[1], w2flat[:, t * N : (t + 1) * N], t * P, (t + 1) * P)
+        for t in range(PACK):
+            acc = product(PACK + t, w2q, slice(t * P, (t + 1) * P), eq)
+            scaled_out(ye[:, t, :], acc, u2[:, t : t + 1], t < 1)
+        hq = mx_tiles("hq")
+        h2q = mx_tiles("h2q")
+        pieces = [(0, 256), (256, 384), (384, 512)]
+        for k, (lo, hi) in enumerate(pieces):
+            for t in range(PACK):
+                neighbours(yr, ye, t, rn_t, lo, hi)
+            hid2 = sb.tile([P, PACK * (hi - lo)], BF16, name="hid2", tag="hid2_%d" % k, align_bytes=64)
+            combine(hid2[:], ye, yr, lo, hi)
+            quantize(h2q[0], h2q[1], hid2[:], lo, hi)
+        hid_first = sb.tile([P, PACK * P], BF16, name="hid_first", tag="ew", align_bytes=64)
+        hid_rest = sb.tile([P, PACK * (N - P)], BF16, name="hid_rest", tag="hid2_0", align_bytes=64)
+
+        def left_chunk(m):
+            grouped = hid_first[:] if m == 0 else hid_rest[:, PACK * P * (m - 1) : PACK * P * m]
+            combine(grouped, y, yl, m * P, (m + 1) * P)
+            quantize(hq[0], hq[1], grouped, m * P, (m + 1) * P)
+
+        left_chunk(0)
+        scores = []
+        for m in range(PACK):
+            if m + 1 < PACK:
+                left_chunk(m + 1)
+            acc = product(m, hq, slice(m * P, (m + 1) * P), h2q)
+            sc_pad = sb.tile([P, N + 32], F32, name="sc%d" % m)
+            nc.gpsimd.memset(sc_pad[:, N:], 0.0)
+            sc = sc_pad[:, :N]
+            if m == 0:
+                nc.scalar.copy(out=sc, in_=acc[:])
+            else:
+                nc.vector.tensor_copy(out=sc, in_=acc[:])
+            shifted = sb.tile([P, N], F32, name="shifted%d" % m)
+            if m < PACK - 1:
+                nc.scalar.activation(shifted[:], sc_pad[:].indirect(dsp_t[:]), COPY, scale=0.8)
+            else:
+                for h in range(2):
+                    cols = slice(h * HALF, (h + 1) * HALF)
+                    nc.scalar.activation(shifted[:, cols], sc_pad[:].indirect(dsp_t[:, h * 16 : (h + 1) * 16]), COPY, scale=0.8)
+            scores.append((acc, shifted))
+        for m, (acc, shifted) in enumerate(scores):
+            res = sb.tile([P, N], F32, name="res%d" % m)
+            parts = 2 if m == PACK - 1 else 1
+            for h in range(parts):
+                cols = slice(h * N // parts, (h + 1) * N // parts)
+                nc.vector.tensor_tensor(out=res[:, cols], in0=shifted[:, cols], in1=acc[:, cols], op=ALU.max)
+                nc.sync.dma_start(out=out[m * P : (m + 1) * P, cols], in_=res[:, cols])

@@ -17,6 +17,7 @@ PACK = 4
 N = 512
 T_LEFT, T_RIGHT = 1024, 2048
 HALF = N // 2
+EARLY = N - P
 FLOPS = 3 * 2 * N * N * N
 
 
@@ -59,7 +60,7 @@ def tile_picked_ystrmat_max_p_kernel(
 
         def load_unit(name, src):
             t = sb.tile([P, PACK], F32, name=name, tag=name, align_bytes=64)
-            nc.gpsimd.dma_start(out=t[:], in_=src.rearrange("(p t) o -> p (t o)", t=PACK))
+            nc.sync.dma_start(out=t[:], in_=src.rearrange("(p t) o -> p (t o)", t=PACK))
             return t
 
         def pick(name, table, lst, dtype, tag):
@@ -96,13 +97,13 @@ def tile_picked_ystrmat_max_p_kernel(
             else:
                 nc.vector.tensor_scalar(out=dst, in0=acc[:], scalar1=factor, scalar2=None, op0=ALU.mult)
 
-        def neighbours(share, planes, t, lst, lo, hi):
-            nc.scalar.activation(share[:, t, lo:hi], planes[:, t, :].indirect(lst[:, lo // 16 : hi // 16]), COPY, scale=-0.6)
+        def neighbours(dst, planes, t, lst, lo, hi):
+            nc.scalar.activation(dst, planes[:, t, :].indirect(lst[:, lo // 16 : hi // 16]), COPY, scale=-0.6)
 
         def combine(grouped, planes, share, lo, hi):
             dst = grouped.rearrange("p (c i t) -> p c t i", i=4, t=PACK)
             a = planes[:, :, lo:hi].rearrange("p t (c i) -> p c t i", i=4)
-            b = share[:, :, lo:hi].rearrange("p t (c i) -> p c t i", i=4)
+            b = share.rearrange("p t (c i) -> p c t i", i=4)
             nc.vector.tensor_tensor(out=dst, in0=a, in1=b, op=ALU.add)
 
         offs_t = load_list("offs_t", offs)
@@ -110,62 +111,67 @@ def tile_picked_ystrmat_max_p_kernel(
         xs = load_scales_spread("xs", x_scales, T_LEFT)
         w1_raw = [load_weight_half("w1_raw%d" % h, w1, h) for h in range(2)]
         u1 = load_unit("u1", unit)
-        u2 = load_unit("u2", unit2)
-        rgt_t = load_list("rgt_t", rgt)
         ln_t = load_list("ln_t", ln)
-        es = load_scales_spread("es", e_scales, T_RIGHT)
+        rgt_t = load_list("rgt_t", rgt)
+        es = load_scales("es", e_scales, T_RIGHT, nc.gpsimd)
         ew = load_words("ew", e_words, T_RIGHT)
         w2_raw = [load_weight_half("w2_raw%d" % h, w2, h) for h in range(2)]
+        u2 = load_unit("u2", unit2)
         rn_t = load_list("rn_t", rn)
         dsp_t = load_list("dsp_t", dsp)
 
         xq = (pick("xq_w", xw, offs_t, U32, "xq_w"), pick("xq_s", xs, offs_t, U8, "xq_s"))
-        w1b = sb.tile([P, PACK, P, PACK], BF16, name="w1b", align_bytes=64)
+        w1b = sb.tile([P, PACK, P, PACK], BF16, name="w1b", tag="w1b", align_bytes=64)
         cast_weight(w1b, w1_raw[0], 0, 0, 64, True)
         cast_weight(w1b, w1_raw[1], 1, 0, 44, False)
         cast_weight(w1b, w1_raw[1], 1, 44, 64, True)
         w1q = mx_tiles("w1q")
         w1flat = w1b[:].rearrange("p t m j -> p (t m j)")
         y_pad = sb.tile([P, (PACK + 1) * N], F32, name="y_pad")
-        nc.gpsimd.memset(y_pad[:, PACK * N :], 0.0)
+        nc.vector.memset(y_pad[:, PACK * N :], 0.0)
         y = y_pad[:, : PACK * N].rearrange("p (t n) -> p t n", t=PACK)
-        yl = sb.tile([P, PACK, N], F32, name="yl")
+        yl = sb.tile([P, PACK, EARLY], F32, name="yl")
         for t in reversed(range(PACK)):
             quantize(w1q[0], w1q[1], w1flat[:, t * N : (t + 1) * N], t * P, (t + 1) * P)
         for t in reversed(range(PACK)):
             acc = product(t, w1q, slice(t * P, (t + 1) * P), xq)
-            scaled_out(y[:, t, :], acc, u1[:, t : t + 1], t == PACK - 1)
+            scaled_out(y[:, t, :], acc, u1[:, t : t + 1], t in (0, PACK - 1))
         for t in reversed(range(PACK)):
-            nc.scalar.activation(yl[:, t, :], y_pad[:, t * N : (t + 2) * N].indirect(ln_t[:]), COPY, scale=-0.6)
+            nc.scalar.activation(yl[:, t, :], y_pad[:, t * N : (t + 2) * N].indirect(ln_t[:, : EARLY // 16]), COPY, scale=-0.6)
 
-        eq = (pick("eq_w", ew, rgt_t, U32, "u1"), pick("eq_s", es, rgt_t, U8, "eq_s"))
+        eq = (pick("eq_w", ew, rgt_t, U32, "u1"), pick("eq_s", es, rgt_t, U8, "w1b"))
         w2b = sb.tile([P, PACK, P, PACK], BF16, name="w2b", tag="ew", align_bytes=64)
         for h in range(2):
             cast_weight(w2b, w2_raw[h], h, 0, 64, False)
         w2q = mx_tiles("w2q")
         w2flat = w2b[:].rearrange("p t m j -> p (t m j)")
         ye = sb.tile([P, PACK, N], F32, name="ye")
-        yr = sb.tile([P, PACK, N], F32, name="yr")
         for t in range(PACK):
             quantize(w2q[0], w2q[1], w2flat[:, t * N : (t + 1) * N], t * P, (t + 1) * P)
         for t in range(PACK):
             acc = product(PACK + t, w2q, slice(t * P, (t + 1) * P), eq)
-            scaled_out(ye[:, t, :], acc, u2[:, t : t + 1], t < 1)
+            scaled_out(ye[:, t, :], acc, u2[:, t : t + 1], False)
         hq = mx_tiles("hq")
         h2q = mx_tiles("h2q")
         pieces = [(0, 256), (256, 384), (384, 512)]
+        yr_halves = [sb.tile([P, PACK, HALF], F32, name="yr", tag=tag, align_bytes=64) for tag in ("yr0", "u2")]
         for k, (lo, hi) in enumerate(pieces):
+            yr = yr_halves[lo // HALF][:, :, lo % HALF : lo % HALF + hi - lo]
             for t in range(PACK):
-                neighbours(yr, ye, t, rn_t, lo, hi)
+                neighbours(yr[:, t, :], ye, t, rn_t, lo, hi)
             hid2 = sb.tile([P, PACK * (hi - lo)], BF16, name="hid2", tag="hid2_%d" % k, align_bytes=64)
             combine(hid2[:], ye, yr, lo, hi)
             quantize(h2q[0], h2q[1], hid2[:], lo, hi)
         hid_first = sb.tile([P, PACK * P], BF16, name="hid_first", tag="ew", align_bytes=64)
-        hid_rest = sb.tile([P, PACK * (N - P)], BF16, name="hid_rest", tag="hid2_0", align_bytes=64)
+        hid_rest = sb.tile([P, PACK * (N - P)], BF16, name="hid_rest", tag="hid2_2", align_bytes=64)
+        yl_late = sb.tile([P, PACK, P], F32, name="yl_late", tag="yr0", align_bytes=64)
+        for t in range(PACK):
+            neighbours(yl_late[:, t, :], y, t, ln_t, EARLY, N)
 
         def left_chunk(m):
             grouped = hid_first[:] if m == 0 else hid_rest[:, PACK * P * (m - 1) : PACK * P * m]
-            combine(grouped, y, yl, m * P, (m + 1) * P)
+            share = yl[:, :, m * P : (m + 1) * P] if m < PACK - 1 else yl_late[:]
+            combine(grouped, y, share, m * P, (m + 1) * P)
             quantize(hq[0], hq[1], grouped, m * P, (m + 1) * P)
 
         left_chunk(0)
@@ -175,7 +181,7 @@ def tile_picked_ystrmat_max_p_kernel(
                 left_chunk(m + 1)
             acc = product(m, hq, slice(m * P, (m + 1) * P), h2q)
             sc_pad = sb.tile([P, N + 32], F32, name="sc%d" % m)
-            nc.gpsimd.memset(sc_pad[:, N:], 0.0)
+            nc.vector.memset(sc_pad[:, N:], 0.0)
             sc = sc_pad[:, :N]
             if m == 0:
                 nc.scalar.copy(out=sc, in_=acc[:])

@@ -41,7 +41,7 @@ def tile_picked_ystrmat_max_p_kernel(
 
         def load_scales(name, src, width, queue):
             t = sb.tile([P, width], U8, name=name, align_bytes=64)
-            nc.gpsimd.memset(t[:].bitcast(I32), 0)
+            nc.vector.memset(t[:].bitcast(I32), 0)
             for q in range(4):
                 queue.dma_start(out=t[32 * q : 32 * q + 4, :].bitcast(I32), in_=src[0, 4 * q : 4 * q + 4, :].bitcast(I32))
             return t
@@ -60,7 +60,7 @@ def tile_picked_ystrmat_max_p_kernel(
 
         def load_unit(name, src):
             t = sb.tile([P, PACK], F32, name=name, tag=name, align_bytes=64)
-            nc.sync.dma_start(out=t[:], in_=src.rearrange("(p t) o -> p (t o)", t=PACK))
+            nc.gpsimd.dma_start(out=t[:], in_=src.rearrange("(p t) o -> p (t o)", t=PACK))
             return t
 
         def pick(name, table, lst, dtype, tag):
@@ -84,11 +84,12 @@ def tile_picked_ystrmat_max_p_kernel(
             scales = sb.tile([P, N], U8, name=name + "_scales", align_bytes=64)
             return codes, scales
 
-        def product(bank, lhs, cols, rhs):
+        def product(bank, lhs, cols, rhs, spans=((0, N),)):
             acc = ps.tile([P, N], F32, name="acc", tag="bank%d" % bank)
-            nc.tensor.matmul_mx(
-                out=acc[:], lhsT=lhs[0][:, cols].bitcast(FP8X4), lhsT_scale=lhs[1][:, cols],
-                rhs=rhs[0][:].bitcast(FP8X4), rhs_scale=rhs[1][:], start=True, stop=True)
+            for lo, hi in spans:
+                nc.tensor.matmul_mx(
+                    out=acc[:, lo:hi], lhsT=lhs[0][:, cols].bitcast(FP8X4), lhsT_scale=lhs[1][:, cols],
+                    rhs=rhs[0][:, lo:hi].bitcast(FP8X4), rhs_scale=rhs[1][:, lo:hi], start=True, stop=True)
             return acc
 
         def scaled_out(dst, acc, factor, on_scalar):
@@ -100,21 +101,21 @@ def tile_picked_ystrmat_max_p_kernel(
         def neighbours(dst, planes, t, lst, lo, hi):
             nc.scalar.activation(dst, planes[:, t, :].indirect(lst[:, lo // 16 : hi // 16]), COPY, scale=-0.6)
 
-        def combine(grouped, planes, share, lo, hi):
+        def combine(engine, grouped, planes, share, lo, hi):
             dst = grouped.rearrange("p (c i t) -> p c t i", i=4, t=PACK)
             a = planes[:, :, lo:hi].rearrange("p t (c i) -> p c t i", i=4)
             b = share.rearrange("p t (c i) -> p c t i", i=4)
-            nc.vector.tensor_tensor(out=dst, in0=a, in1=b, op=ALU.add)
+            engine.tensor_tensor(out=dst, in0=a, in1=b, op=ALU.add)
 
         offs_t = load_list("offs_t", offs)
         xw = load_words("xw", x_words, T_LEFT)
         xs = load_scales_spread("xs", x_scales, T_LEFT)
         w1_raw = [load_weight_half("w1_raw%d" % h, w1, h) for h in range(2)]
         u1 = load_unit("u1", unit)
-        ln_t = load_list("ln_t", ln)
         rgt_t = load_list("rgt_t", rgt)
-        es = load_scales("es", e_scales, T_RIGHT, nc.gpsimd)
+        es = load_scales("es", e_scales, T_RIGHT, nc.sync)
         ew = load_words("ew", e_words, T_RIGHT)
+        ln_t = load_list("ln_t", ln)
         w2_raw = [load_weight_half("w2_raw%d" % h, w2, h) for h in range(2)]
         u2 = load_unit("u2", unit2)
         rn_t = load_list("rn_t", rn)
@@ -135,11 +136,11 @@ def tile_picked_ystrmat_max_p_kernel(
             quantize(w1q[0], w1q[1], w1flat[:, t * N : (t + 1) * N], t * P, (t + 1) * P)
         for t in reversed(range(PACK)):
             acc = product(t, w1q, slice(t * P, (t + 1) * P), xq)
-            scaled_out(y[:, t, :], acc, u1[:, t : t + 1], t in (0, PACK - 1))
+            scaled_out(y[:, t, :], acc, u1[:, t : t + 1], t != 1)
         for t in reversed(range(PACK)):
             nc.scalar.activation(yl[:, t, :], y_pad[:, t * N : (t + 2) * N].indirect(ln_t[:, : EARLY // 16]), COPY, scale=-0.6)
 
-        eq = (pick("eq_w", ew, rgt_t, U32, "u1"), pick("eq_s", es, rgt_t, U8, "w1b"))
+        eq = (pick("eq_w", ew, rgt_t, U32, "xq_w"), pick("eq_s", es, rgt_t, U8, "w1b"))
         w2b = sb.tile([P, PACK, P, PACK], BF16, name="w2b", tag="ew", align_bytes=64)
         for h in range(2):
             cast_weight(w2b, w2_raw[h], h, 0, 64, False)
@@ -160,9 +161,9 @@ def tile_picked_ystrmat_max_p_kernel(
             for t in range(PACK):
                 neighbours(yr[:, t, :], ye, t, rn_t, lo, hi)
             hid2 = sb.tile([P, PACK * (hi - lo)], BF16, name="hid2", tag="hid2_%d" % k, align_bytes=64)
-            combine(hid2[:], ye, yr, lo, hi)
+            combine(nc.vector, hid2[:], ye, yr, lo, hi)
             quantize(h2q[0], h2q[1], hid2[:], lo, hi)
-        hid_first = sb.tile([P, PACK * P], BF16, name="hid_first", tag="ew", align_bytes=64)
+        hid_first = sb.tile([P, PACK * P], BF16, name="hid_first", tag="xq_w", align_bytes=64)
         hid_rest = sb.tile([P, PACK * (N - P)], BF16, name="hid_rest", tag="hid2_2", align_bytes=64)
         yl_late = sb.tile([P, PACK, P], F32, name="yl_late", tag="yr0", align_bytes=64)
         for t in range(PACK):
@@ -171,7 +172,7 @@ def tile_picked_ystrmat_max_p_kernel(
         def left_chunk(m):
             grouped = hid_first[:] if m == 0 else hid_rest[:, PACK * P * (m - 1) : PACK * P * m]
             share = yl[:, :, m * P : (m + 1) * P] if m < PACK - 1 else yl_late[:]
-            combine(grouped, y, share, m * P, (m + 1) * P)
+            combine(nc.vector, grouped, y, share, m * P, (m + 1) * P)
             quantize(hq[0], hq[1], grouped, m * P, (m + 1) * P)
 
         left_chunk(0)
@@ -179,14 +180,18 @@ def tile_picked_ystrmat_max_p_kernel(
         for m in range(PACK):
             if m + 1 < PACK:
                 left_chunk(m + 1)
-            acc = product(m, hq, slice(m * P, (m + 1) * P), h2q)
+            rows = slice(m * P, (m + 1) * P)
             sc_pad = sb.tile([P, N + 32], F32, name="sc%d" % m)
             nc.vector.memset(sc_pad[:, N:], 0.0)
-            sc = sc_pad[:, :N]
             if m == 0:
-                nc.scalar.copy(out=sc, in_=acc[:])
+                split = pieces[-1][0]
+                banks = [(product(0, hq, rows, h2q, pieces[:-1]), slice(0, split)), (product(PACK, hq, rows, h2q, pieces[-1:]), slice(split, N))]
+                for acc, cols in banks:
+                    nc.scalar.copy(out=sc_pad[:, cols], in_=acc[:, cols])
             else:
-                nc.vector.tensor_copy(out=sc, in_=acc[:])
+                acc = product(m, hq, rows, h2q)
+                nc.vector.tensor_copy(out=sc_pad[:, :N], in_=acc[:])
+                banks = [(acc, slice(0, N))] if m < PACK - 1 else [(acc, slice(0, HALF)), (acc, slice(HALF, N))]
             shifted = sb.tile([P, N], F32, name="shifted%d" % m)
             if m < PACK - 1:
                 nc.scalar.activation(shifted[:], sc_pad[:].indirect(dsp_t[:]), COPY, scale=0.8)
@@ -194,11 +199,12 @@ def tile_picked_ystrmat_max_p_kernel(
                 for h in range(2):
                     cols = slice(h * HALF, (h + 1) * HALF)
                     nc.scalar.activation(shifted[:, cols], sc_pad[:].indirect(dsp_t[:, h * 16 : (h + 1) * 16]), COPY, scale=0.8)
-            scores.append((acc, shifted))
-        for m, (acc, shifted) in enumerate(scores):
+            scores.append((banks, shifted))
+        for m, (banks, shifted) in enumerate(scores):
             res = sb.tile([P, N], F32, name="res%d" % m)
-            parts = 2 if m == PACK - 1 else 1
-            for h in range(parts):
-                cols = slice(h * N // parts, (h + 1) * N // parts)
+            for acc, cols in banks:
                 nc.vector.tensor_tensor(out=res[:, cols], in0=shifted[:, cols], in1=acc[:, cols], op=ALU.max)
-                nc.sync.dma_start(out=out[m * P : (m + 1) * P, cols], in_=res[:, cols])
+                if m == PACK - 1:
+                    nc.sync.dma_start(out=out[m * P : (m + 1) * P, cols], in_=res[:, cols])
+            if m < PACK - 1:
+                nc.sync.dma_start(out=out[m * P : (m + 1) * P, :], in_=res[:])

@@ -79,8 +79,8 @@ def tile_picked_ystrmat_max_p_kernel(
         def quantize(codes, scales, grouped, lo, hi):
             nc.vector.quantize_mx(out=codes[:, lo:hi].bitcast(FP8X4), scales=scales[:, lo:hi], in_=grouped)
 
-        def mx_tiles(name):
-            codes = sb.tile([P, N], U32, name=name + "_codes", align_bytes=64)
+        def mx_tiles(name, tag=""):
+            codes = sb.tile([P, N], U32, name=name + "_codes", tag=tag or name, align_bytes=64)
             scales = sb.tile([P, N], U8, name=name + "_scales", align_bytes=64)
             return codes, scales
 
@@ -152,7 +152,7 @@ def tile_picked_ystrmat_max_p_kernel(
         for t in range(PACK):
             acc = product(PACK + t, w2q, slice(t * P, (t + 1) * P), eq)
             scaled_out(ye[:, t, :], acc, u2[:, t : t + 1], False)
-        hq = mx_tiles("hq")
+        hq = mx_tiles("hq", "xq_w")
         h2q = mx_tiles("h2q")
         pieces = [(0, 256), (256, 384), (384, 512)]
         yr_halves = [sb.tile([P, PACK, HALF], F32, name="yr", tag=tag, align_bytes=64) for tag in ("yr0", "u2")]
@@ -163,23 +163,28 @@ def tile_picked_ystrmat_max_p_kernel(
             hid2 = sb.tile([P, PACK * (hi - lo)], BF16, name="hid2", tag="hid2_%d" % k, align_bytes=64)
             combine(nc.vector, hid2[:], ye, yr, lo, hi)
             quantize(h2q[0], h2q[1], hid2[:], lo, hi)
-        hid_first = sb.tile([P, PACK * P], BF16, name="hid_first", tag="xq_w", align_bytes=64)
-        hid_rest = sb.tile([P, PACK * (N - P)], BF16, name="hid_rest", tag="hid2_2", align_bytes=64)
         yl_late = sb.tile([P, PACK, P], F32, name="yl_late", tag="yr0", align_bytes=64)
         for t in range(PACK):
             neighbours(yl_late[:, t, :], y, t, ln_t, EARLY, N)
 
         def left_chunk(m):
-            grouped = hid_first[:] if m == 0 else hid_rest[:, PACK * P * (m - 1) : PACK * P * m]
+            tag = ("hid0", "w1b", "hid2_2", "hid2_2")[m]
+            grouped = sb.tile([P, PACK * P], BF16, name="hid", tag=tag, align_bytes=64)
             share = yl[:, :, m * P : (m + 1) * P] if m < PACK - 1 else yl_late[:]
-            combine(nc.vector, grouped, y, share, m * P, (m + 1) * P)
-            quantize(hq[0], hq[1], grouped, m * P, (m + 1) * P)
+            combine(nc.gpsimd if m in (0, PACK - 1) else nc.vector, grouped[:], y, share, m * P, (m + 1) * P)
+            return grouped
 
-        left_chunk(0)
+        def left_codes(m, grouped):
+            quantize(hq[0], hq[1], grouped[:], m * P, (m + 1) * P)
+
+        early = [left_chunk(m) for m in range(2)]
+        for m, grouped in enumerate(early):
+            left_codes(m, grouped)
+        left_codes(2, left_chunk(2))
         scores = []
         for m in range(PACK):
-            if m + 1 < PACK:
-                left_chunk(m + 1)
+            if m == PACK - 1:
+                left_codes(m, left_chunk(m))
             rows = slice(m * P, (m + 1) * P)
             sc_pad = sb.tile([P, N + 32], F32, name="sc%d" % m)
             nc.vector.memset(sc_pad[:, N:], 0.0)
@@ -201,7 +206,7 @@ def tile_picked_ystrmat_max_p_kernel(
                     nc.scalar.activation(shifted[:, cols], sc_pad[:].indirect(dsp_t[:, h * 16 : (h + 1) * 16]), COPY, scale=0.8)
             scores.append((banks, shifted))
         for m, (banks, shifted) in enumerate(scores):
-            res = sb.tile([P, N], F32, name="res%d" % m)
+            res = sb.tile([P, N], F32, name="res", tag=("hid2_2", "h2q", "xq_w", "res3")[m], align_bytes=64)
             for acc, cols in banks:
                 nc.vector.tensor_tensor(out=res[:, cols], in0=shifted[:, cols], in1=acc[:, cols], op=ALU.max)
                 if m == PACK - 1:

@@ -15,9 +15,19 @@ ALU = mybir.AluOpType
 P = 128
 PACK = 4
 N = 512
-T_LEFT, T_RIGHT = 1024, 2048
 HALF = N // 2
+T_LEFT, T_RIGHT = 1024, 2048
+PER_COLUMN = 16
+QUADRANT = 32
+LINE = 4
+NEIGHBOUR, DISPARITY = -0.6, 0.8
+
+M_HALF = P // 2
+M_VECTOR = 44
 EARLY = N - P
+PIECES = [(0, 256), (256, 384), (384, 512)]
+SPARE = 32
+
 FLOPS = 3 * 2 * N * N * N
 
 
@@ -30,90 +40,96 @@ def tile_picked_ystrmat_max_p_kernel(
         ps = ctx.enter_context(tc.psum_pool(name="ps", bufs=1))
 
         def load_list(name, src):
-            t = sb.tile([P, N // 16], U16, name=name)
-            nc.sync.dma_start(t[:], src)
-            return t
+            entries = sb.tile([P, N // PER_COLUMN], U16, name=name)
+            nc.sync.dma_start(entries[:], src)
+            return entries
 
         def load_words(name, src, width):
-            t = sb.tile([P, width], U32, name=name, tag=name, align_bytes=64)
-            nc.sync.dma_start(out=t[:].bitcast(I32), in_=src[0].rearrange("p n t -> p (n t)").bitcast(I32))
-            return t
+            words = sb.tile([P, width], U32, name=name, tag=name, align_bytes=64)
+            nc.sync.dma_start(out=words[:].bitcast(I32), in_=src[0].rearrange("p n t -> p (n t)").bitcast(I32))
+            return words
 
-        def load_scales(name, src, width, queue):
-            t = sb.tile([P, width], U8, name=name, align_bytes=64)
-            nc.vector.memset(t[:].bitcast(I32), 0)
-            for q in range(4):
-                queue.dma_start(out=t[32 * q : 32 * q + 4, :].bitcast(I32), in_=src[0, 4 * q : 4 * q + 4, :].bitcast(I32))
-            return t
+        def load_scales_repeated(name, src, width):
+            table = sb.tile([P, width], U8, name=name, align_bytes=64)
+            for q in range(P // QUADRANT):
+                rows = src[0, PACK * q : PACK * (q + 1), :].bitcast(I32)
+                dst = table[QUADRANT * q : QUADRANT * (q + 1), :].bitcast(I32)
+                nc.sync.dma_start(out=dst, in_=rows.partition_broadcast(QUADRANT // PACK))
+            return table
 
-        def load_scales_spread(name, src, width):
-            t = sb.tile([P, width], U8, name=name, align_bytes=64)
-            for q in range(4):
-                rows = src[0, 4 * q : 4 * q + 4, :].bitcast(I32)
-                nc.sync.dma_start(out=t[32 * q : 32 * q + 32, :].bitcast(I32), in_=rows.partition_broadcast(8))
-            return t
+        def load_scales_cleared(name, src, width):
+            table = sb.tile([P, width], U8, name=name, align_bytes=64)
+            nc.vector.memset(table[:].bitcast(I32), 0)
+            for q in range(P // QUADRANT):
+                dst = table[QUADRANT * q : QUADRANT * q + PACK, :].bitcast(I32)
+                nc.sync.dma_start(out=dst, in_=src[0, PACK * q : PACK * (q + 1), :].bitcast(I32))
+            return table
 
         def load_weight_half(name, src, h):
-            t = sb.tile([P, PACK, HALF], F32, name=name)
-            nc.sync.dma_start(out=t[:], in_=src.rearrange("(p j) c -> p j c", j=PACK)[:, :, h * HALF : (h + 1) * HALF])
-            return t
+            raw = sb.tile([P, PACK, HALF], F32, name=name)
+            nc.sync.dma_start(out=raw[:], in_=src.rearrange("(p j) c -> p j c", j=PACK)[:, :, h * HALF : (h + 1) * HALF])
+            return raw
 
         def load_unit(name, src):
-            t = sb.tile([P, PACK], F32, name=name, tag=name, align_bytes=64)
-            nc.gpsimd.dma_start(out=t[:], in_=src.rearrange("(p t) o -> p (t o)", t=PACK))
-            return t
+            factors = sb.tile([P, PACK], F32, name=name, tag=name, align_bytes=64)
+            nc.gpsimd.dma_start(out=factors[:], in_=src.rearrange("(p t) o -> p (t o)", t=PACK))
+            return factors
 
-        def pick(name, table, lst, dtype, tag):
-            t = sb.tile([P, N], dtype, name=name, tag=tag, align_bytes=64)
-            nc.vector.tensor_copy(t[:], table[:].indirect(lst[:]))
-            return t
+        def pick(name, table, entries, dtype, tag):
+            picked = sb.tile([P, N], dtype, name=name, tag=tag, align_bytes=64)
+            nc.vector.tensor_copy(picked[:], table[:].indirect(entries[:]))
+            return picked
 
-        def cast_weight(wb, raw, h, lo, hi, on_scalar):
-            dst = wb[:, :, h * 64 + lo : h * 64 + hi, :].rearrange("p t m j -> p m j t")
+        def round_weight(copy, dealt, raw, h, lo, hi):
+            dst = dealt[:, :, h * M_HALF + lo : h * M_HALF + hi, :].rearrange("p t m j -> p m j t")
             src = raw[:, :, PACK * lo : PACK * hi].rearrange("p j (m t) -> p m j t", t=PACK)
-            if on_scalar:
-                nc.scalar.copy(out=dst, in_=src)
-            else:
-                nc.vector.tensor_copy(out=dst, in_=src)
+            copy(out=dst, in_=src)
 
-        def quantize(codes, scales, grouped, lo, hi):
-            nc.vector.quantize_mx(out=codes[:, lo:hi].bitcast(FP8X4), scales=scales[:, lo:hi], in_=grouped)
-
-        def mx_tiles(name, tag=""):
-            codes = sb.tile([P, N], U32, name=name + "_codes", tag=tag or name, align_bytes=64)
+        def mx_tiles(name, tag):
+            codes = sb.tile([P, N], U32, name=name + "_codes", tag=tag, align_bytes=64)
             scales = sb.tile([P, N], U8, name=name + "_scales", align_bytes=64)
             return codes, scales
 
-        def product(bank, lhs, cols, rhs, spans=((0, N),)):
+        def quantize(operand, grouped, lo, hi):
+            codes, scales = operand
+            nc.vector.quantize_mx(out=codes[:, lo:hi].bitcast(FP8X4), scales=scales[:, lo:hi], in_=grouped)
+
+        def quantize_weight_plane(operand, dealt, t):
+            flat = dealt[:].rearrange("p t m j -> p (t m j)")
+            quantize(operand, flat[:, t * N : (t + 1) * N], t * P, (t + 1) * P)
+
+        def product(bank, lhs, block, rhs, spans):
             acc = ps.tile([P, N], F32, name="acc", tag="bank%d" % bank)
+            cols = slice(block * P, (block + 1) * P)
             for lo, hi in spans:
                 nc.tensor.matmul_mx(
-                    out=acc[:, lo:hi], lhsT=lhs[0][:, cols].bitcast(FP8X4), lhsT_scale=lhs[1][:, cols],
-                    rhs=rhs[0][:, lo:hi].bitcast(FP8X4), rhs_scale=rhs[1][:, lo:hi], start=True, stop=True)
+                    out=acc[:, lo:hi],
+                    lhsT=lhs[0][:, cols].bitcast(FP8X4),
+                    lhsT_scale=lhs[1][:, cols],
+                    rhs=rhs[0][:, lo:hi].bitcast(FP8X4),
+                    rhs_scale=rhs[1][:, lo:hi],
+                    start=True,
+                    stop=True,
+                )
             return acc
 
-        def scaled_out(dst, acc, factor, on_scalar):
-            if on_scalar:
-                nc.scalar.activation(dst, acc[:], COPY, scale=factor)
-            else:
-                nc.vector.tensor_scalar(out=dst, in0=acc[:], scalar1=factor, scalar2=None, op0=ALU.mult)
-
-        def neighbours(dst, planes, t, lst, lo, hi):
-            nc.scalar.activation(dst, planes[:, t, :].indirect(lst[:, lo // 16 : hi // 16]), COPY, scale=-0.6)
+        def fetch(dst, window, entries, lo, hi, factor):
+            nc.scalar.activation(dst, window.indirect(entries[:, lo // PER_COLUMN : hi // PER_COLUMN]), COPY, scale=factor)
 
         def combine(engine, grouped, planes, share, lo, hi):
-            dst = grouped.rearrange("p (c i t) -> p c t i", i=4, t=PACK)
-            a = planes[:, :, lo:hi].rearrange("p t (c i) -> p c t i", i=4)
-            b = share.rearrange("p t (c i) -> p c t i", i=4)
-            engine.tensor_tensor(out=dst, in0=a, in1=b, op=ALU.add)
+            dst = grouped.rearrange("p (c i t) -> p c t i", i=LINE, t=PACK)
+            own = planes[:, :, lo:hi].rearrange("p t (c i) -> p c t i", i=LINE)
+            engine.tensor_tensor(out=dst, in0=own, in1=share.rearrange("p t (c i) -> p c t i", i=LINE), op=ALU.add)
+
+        whole = [(0, N)]
 
         offs_t = load_list("offs_t", offs)
         xw = load_words("xw", x_words, T_LEFT)
-        xs = load_scales_spread("xs", x_scales, T_LEFT)
+        xs = load_scales_repeated("xs", x_scales, T_LEFT)
         w1_raw = [load_weight_half("w1_raw%d" % h, w1, h) for h in range(2)]
         u1 = load_unit("u1", unit)
         rgt_t = load_list("rgt_t", rgt)
-        es = load_scales("es", e_scales, T_RIGHT, nc.sync)
+        es = load_scales_cleared("es", e_scales, T_RIGHT)
         ew = load_words("ew", e_words, T_RIGHT)
         ln_t = load_list("ln_t", ln)
         w2_raw = [load_weight_half("w2_raw%d" % h, w2, h) for h in range(2)]
@@ -123,93 +139,101 @@ def tile_picked_ystrmat_max_p_kernel(
 
         xq = (pick("xq_w", xw, offs_t, U32, "xq_w"), pick("xq_s", xs, offs_t, U8, "xq_s"))
         w1b = sb.tile([P, PACK, P, PACK], BF16, name="w1b", tag="w1b", align_bytes=64)
-        cast_weight(w1b, w1_raw[0], 0, 0, 64, True)
-        cast_weight(w1b, w1_raw[1], 1, 0, 44, False)
-        cast_weight(w1b, w1_raw[1], 1, 44, 64, True)
-        w1q = mx_tiles("w1q")
-        w1flat = w1b[:].rearrange("p t m j -> p (t m j)")
+        round_weight(nc.scalar.copy, w1b, w1_raw[0], 0, 0, M_HALF)
+        round_weight(nc.vector.tensor_copy, w1b, w1_raw[1], 1, 0, M_VECTOR)
+        round_weight(nc.scalar.copy, w1b, w1_raw[1], 1, M_VECTOR, M_HALF)
+        w1q = mx_tiles("w1q", "w1q")
         y_pad = sb.tile([P, (PACK + 1) * N], F32, name="y_pad")
         nc.vector.memset(y_pad[:, PACK * N :], 0.0)
         y = y_pad[:, : PACK * N].rearrange("p (t n) -> p t n", t=PACK)
         yl = sb.tile([P, PACK, EARLY], F32, name="yl")
         for t in reversed(range(PACK)):
-            quantize(w1q[0], w1q[1], w1flat[:, t * N : (t + 1) * N], t * P, (t + 1) * P)
+            quantize_weight_plane(w1q, w1b, t)
         for t in reversed(range(PACK)):
-            acc = product(t, w1q, slice(t * P, (t + 1) * P), xq)
-            scaled_out(y[:, t, :], acc, u1[:, t : t + 1], t != 1)
+            acc = product(t, w1q, t, xq, whole)
+            if t == 1:
+                nc.vector.tensor_scalar(out=y[:, t, :], in0=acc[:], scalar1=u1[:, t : t + 1], scalar2=None, op0=ALU.mult)
+            else:
+                nc.scalar.activation(y[:, t, :], acc[:], COPY, scale=u1[:, t : t + 1])
         for t in reversed(range(PACK)):
-            nc.scalar.activation(yl[:, t, :], y_pad[:, t * N : (t + 2) * N].indirect(ln_t[:, : EARLY // 16]), COPY, scale=-0.6)
+            fetch(yl[:, t, :], y_pad[:, t * N : (t + 2) * N], ln_t, 0, EARLY, NEIGHBOUR)
 
         eq = (pick("eq_w", ew, rgt_t, U32, "xq_w"), pick("eq_s", es, rgt_t, U8, "w1b"))
         w2b = sb.tile([P, PACK, P, PACK], BF16, name="w2b", tag="ew", align_bytes=64)
         for h in range(2):
-            cast_weight(w2b, w2_raw[h], h, 0, 64, False)
-        w2q = mx_tiles("w2q")
-        w2flat = w2b[:].rearrange("p t m j -> p (t m j)")
+            round_weight(nc.vector.tensor_copy, w2b, w2_raw[h], h, 0, M_HALF)
+        w2q = mx_tiles("w2q", "w2q")
         ye = sb.tile([P, PACK, N], F32, name="ye")
         for t in range(PACK):
-            quantize(w2q[0], w2q[1], w2flat[:, t * N : (t + 1) * N], t * P, (t + 1) * P)
+            quantize_weight_plane(w2q, w2b, t)
         for t in range(PACK):
-            acc = product(PACK + t, w2q, slice(t * P, (t + 1) * P), eq)
-            scaled_out(ye[:, t, :], acc, u2[:, t : t + 1], False)
+            acc = product(PACK + t, w2q, t, eq, whole)
+            nc.vector.tensor_scalar(out=ye[:, t, :], in0=acc[:], scalar1=u2[:, t : t + 1], scalar2=None, op0=ALU.mult)
         hq = mx_tiles("hq", "xq_w")
-        h2q = mx_tiles("h2q")
-        pieces = [(0, 256), (256, 384), (384, 512)]
+        h2q = mx_tiles("h2q", "h2q")
         yr_halves = [sb.tile([P, PACK, HALF], F32, name="yr", tag=tag, align_bytes=64) for tag in ("yr0", "u2")]
-        for k, (lo, hi) in enumerate(pieces):
+        for k, (lo, hi) in enumerate(PIECES):
             yr = yr_halves[lo // HALF][:, :, lo % HALF : lo % HALF + hi - lo]
             for t in range(PACK):
-                neighbours(yr[:, t, :], ye, t, rn_t, lo, hi)
+                fetch(yr[:, t, :], ye[:, t, :], rn_t, lo, hi, NEIGHBOUR)
             hid2 = sb.tile([P, PACK * (hi - lo)], BF16, name="hid2", tag="hid2_%d" % k, align_bytes=64)
             combine(nc.vector, hid2[:], ye, yr, lo, hi)
-            quantize(h2q[0], h2q[1], hid2[:], lo, hi)
+            quantize(h2q, hid2[:], lo, hi)
+
         yl_late = sb.tile([P, PACK, P], F32, name="yl_late", tag="yr0", align_bytes=64)
         for t in range(PACK):
-            neighbours(yl_late[:, t, :], y, t, ln_t, EARLY, N)
+            fetch(yl_late[:, t, :], y[:, t, :], ln_t, EARLY, N, NEIGHBOUR)
 
-        def left_chunk(m):
-            tag = ("hid0", "w1b", "hid2_2", "hid2_2")[m]
-            grouped = sb.tile([P, PACK * P], BF16, name="hid", tag=tag, align_bytes=64)
-            share = yl[:, :, m * P : (m + 1) * P] if m < PACK - 1 else yl_late[:]
-            combine(nc.gpsimd if m in (0, PACK - 1) else nc.vector, grouped[:], y, share, m * P, (m + 1) * P)
-            return grouped
+        hid_0 = sb.tile([P, PACK * P], BF16, name="hid_0", align_bytes=64)
+        hid_1 = sb.tile([P, PACK * P], BF16, name="hid_1", tag="w1b", align_bytes=64)
+        hid_23 = sb.tile([P, 2 * PACK * P], BF16, name="hid_23", tag="hid2_2", align_bytes=64)
+        hid = [hid_0[:], hid_1[:], hid_23[:, : PACK * P], hid_23[:, PACK * P :]]
+        last = PACK - 1
 
-        def left_codes(m, grouped):
-            quantize(hq[0], hq[1], grouped[:], m * P, (m + 1) * P)
+        def add_chunk(m):
+            share = yl_late[:] if m == last else yl[:, :, m * P : (m + 1) * P]
+            combine(nc.gpsimd if m in (0, last) else nc.vector, hid[m], y, share, m * P, (m + 1) * P)
 
-        early = [left_chunk(m) for m in range(2)]
-        for m, grouped in enumerate(early):
-            left_codes(m, grouped)
-        left_codes(2, left_chunk(2))
+        def quantize_chunk(m):
+            quantize(hq, hid[m], m * P, (m + 1) * P)
+
+        add_chunk(0)
+        add_chunk(1)
+        quantize_chunk(0)
+        quantize_chunk(1)
+        add_chunk(2)
+        quantize_chunk(2)
+
         scores = []
         for m in range(PACK):
-            if m == PACK - 1:
-                left_codes(m, left_chunk(m))
-            rows = slice(m * P, (m + 1) * P)
-            sc_pad = sb.tile([P, N + 32], F32, name="sc%d" % m)
-            nc.vector.memset(sc_pad[:, N:], 0.0)
+            if m == last:
+                add_chunk(m)
+                quantize_chunk(m)
+            sc = sb.tile([P, N + SPARE], F32, name="sc%d" % m)
+            nc.vector.memset(sc[:, N:], 0.0)
             if m == 0:
-                split = pieces[-1][0]
-                banks = [(product(0, hq, rows, h2q, pieces[:-1]), slice(0, split)), (product(PACK, hq, rows, h2q, pieces[-1:]), slice(split, N))]
-                for acc, cols in banks:
-                    nc.scalar.copy(out=sc_pad[:, cols], in_=acc[:, cols])
+                split = PIECES[-1][0]
+                parts = [
+                    (product(0, hq, m, h2q, PIECES[:-1]), slice(0, split)),
+                    (product(PACK, hq, m, h2q, PIECES[-1:]), slice(split, N)),
+                ]
+                for acc, cols in parts:
+                    nc.scalar.copy(out=sc[:, cols], in_=acc[:, cols])
             else:
-                acc = product(m, hq, rows, h2q)
-                nc.vector.tensor_copy(out=sc_pad[:, :N], in_=acc[:])
-                banks = [(acc, slice(0, N))] if m < PACK - 1 else [(acc, slice(0, HALF)), (acc, slice(HALF, N))]
+                acc = product(m, hq, m, h2q, whole)
+                nc.vector.tensor_copy(out=sc[:, :N], in_=acc[:])
+                parts = [(acc, slice(0, HALF)), (acc, slice(HALF, N))] if m == last else [(acc, slice(0, N))]
             shifted = sb.tile([P, N], F32, name="shifted%d" % m)
-            if m < PACK - 1:
-                nc.scalar.activation(shifted[:], sc_pad[:].indirect(dsp_t[:]), COPY, scale=0.8)
-            else:
-                for h in range(2):
-                    cols = slice(h * HALF, (h + 1) * HALF)
-                    nc.scalar.activation(shifted[:, cols], sc_pad[:].indirect(dsp_t[:, h * 16 : (h + 1) * 16]), COPY, scale=0.8)
-            scores.append((banks, shifted))
-        for m, (banks, shifted) in enumerate(scores):
+            for lo, hi in [(0, HALF), (HALF, N)] if m == last else whole:
+                fetch(shifted[:, lo:hi], sc[:], dsp_t, lo, hi, DISPARITY)
+            scores.append((parts, shifted))
+
+        for m, (parts, shifted) in enumerate(scores):
+            rows = slice(m * P, (m + 1) * P)
             res = sb.tile([P, N], F32, name="res", tag=("hid2_2", "h2q", "xq_w", "res3")[m], align_bytes=64)
-            for acc, cols in banks:
+            for acc, cols in parts:
                 nc.vector.tensor_tensor(out=res[:, cols], in0=shifted[:, cols], in1=acc[:, cols], op=ALU.max)
-                if m == PACK - 1:
-                    nc.sync.dma_start(out=out[m * P : (m + 1) * P, cols], in_=res[:, cols])
-            if m < PACK - 1:
-                nc.sync.dma_start(out=out[m * P : (m + 1) * P, :], in_=res[:])
+                if m == last:
+                    nc.sync.dma_start(out=out[rows, cols], in_=res[:, cols])
+            if m != last:
+                nc.sync.dma_start(out=out[rows, :], in_=res[:])

from contextlib import ExitStack

import concourse.mybir as mybir

F32 = mybir.dt.float32
BF16 = mybir.dt.bfloat16
I32 = mybir.dt.int32
U32 = mybir.dt.uint32
U16 = mybir.dt.uint16
U8 = mybir.dt.uint8
FP8X4 = mybir.dt.float8_e4m3fn_x4
COPY = mybir.ActivationFunctionType.Copy
ALU = mybir.AluOpType

P = 128
PACK = 4
N = 512
HALF = N // 2
T_LEFT, T_RIGHT = 1024, 2048
PER_COLUMN = 16
QUADRANT = 32
LINE = 4
NEIGHBOUR, DISPARITY = -0.6, 0.8

M_HALF = P // 2
M_VECTOR = 44
EARLY = N - P
PIECES = [(0, 256), (256, 384), (384, 512)]
SPARE = 32

FLOPS = 3 * 2 * N * N * N


def tile_picked_ystrmat_max_p_kernel(
    tc, x_words, x_scales, w1, e_words, e_scales, w2, unit, unit2, offs, rgt, ln, rn, dsp, out
):
    nc = tc.nc
    with ExitStack() as ctx:
        sb = ctx.enter_context(tc.tile_pool(name="sb", bufs=1))
        ps = ctx.enter_context(tc.psum_pool(name="ps", bufs=1))

        def load_list(name, src):
            entries = sb.tile([P, N // PER_COLUMN], U16, name=name)
            nc.sync.dma_start(entries[:], src)
            return entries

        def load_words(name, src, width):
            words = sb.tile([P, width], U32, name=name, tag=name, align_bytes=64)
            nc.sync.dma_start(out=words[:].bitcast(I32), in_=src[0].rearrange("p n t -> p (n t)").bitcast(I32))
            return words

        def load_scales_repeated(name, src, width):
            table = sb.tile([P, width], U8, name=name, align_bytes=64)
            for q in range(P // QUADRANT):
                rows = src[0, PACK * q : PACK * (q + 1), :].bitcast(I32)
                dst = table[QUADRANT * q : QUADRANT * (q + 1), :].bitcast(I32)
                nc.sync.dma_start(out=dst, in_=rows.partition_broadcast(QUADRANT // PACK))
            return table

        def load_scales_cleared(name, src, width):
            table = sb.tile([P, width], U8, name=name, align_bytes=64)
            nc.vector.memset(table[:].bitcast(I32), 0)
            for q in range(P // QUADRANT):
                dst = table[QUADRANT * q : QUADRANT * q + PACK, :].bitcast(I32)
                nc.sync.dma_start(out=dst, in_=src[0, PACK * q : PACK * (q + 1), :].bitcast(I32))
            return table

        def load_weight_half(name, src, h):
            raw = sb.tile([P, PACK, HALF], F32, name=name)
            nc.sync.dma_start(out=raw[:], in_=src.rearrange("(p j) c -> p j c", j=PACK)[:, :, h * HALF : (h + 1) * HALF])
            return raw

        def load_unit(name, src):
            factors = sb.tile([P, PACK], F32, name=name, tag=name, align_bytes=64)
            nc.gpsimd.dma_start(out=factors[:], in_=src.rearrange("(p t) o -> p (t o)", t=PACK))
            return factors

        def pick(name, table, entries, dtype, tag):
            picked = sb.tile([P, N], dtype, name=name, tag=tag, align_bytes=64)
            nc.vector.tensor_copy(picked[:], table[:].indirect(entries[:]))
            return picked

        def round_weight(copy, dealt, raw, h, lo, hi):
            dst = dealt[:, :, h * M_HALF + lo : h * M_HALF + hi, :].rearrange("p t m j -> p m j t")
            src = raw[:, :, PACK * lo : PACK * hi].rearrange("p j (m t) -> p m j t", t=PACK)
            copy(out=dst, in_=src)

        def mx_tiles(name, tag):
            codes = sb.tile([P, N], U32, name=name + "_codes", tag=tag, align_bytes=64)
            scales = sb.tile([P, N], U8, name=name + "_scales", align_bytes=64)
            return codes, scales

        def quantize(operand, grouped, lo, hi):
            codes, scales = operand
            nc.vector.quantize_mx(out=codes[:, lo:hi].bitcast(FP8X4), scales=scales[:, lo:hi], in_=grouped)

        def quantize_weight_plane(operand, dealt, t):
            flat = dealt[:].rearrange("p t m j -> p (t m j)")
            quantize(operand, flat[:, t * N : (t + 1) * N], t * P, (t + 1) * P)

        def product(bank, lhs, block, rhs, spans):
            acc = ps.tile([P, N], F32, name="acc", tag="bank%d" % bank)
            cols = slice(block * P, (block + 1) * P)
            for lo, hi in spans:
                nc.tensor.matmul_mx(
                    out=acc[:, lo:hi],
                    lhsT=lhs[0][:, cols].bitcast(FP8X4),
                    lhsT_scale=lhs[1][:, cols],
                    rhs=rhs[0][:, lo:hi].bitcast(FP8X4),
                    rhs_scale=rhs[1][:, lo:hi],
                    start=True,
                    stop=True,
                )
            return acc

        def fetch(dst, window, entries, lo, hi, factor):
            nc.scalar.activation(dst, window.indirect(entries[:, lo // PER_COLUMN : hi // PER_COLUMN]), COPY, scale=factor)

        def combine(engine, grouped, planes, share, lo, hi):
            dst = grouped.rearrange("p (c i t) -> p c t i", i=LINE, t=PACK)
            own = planes[:, :, lo:hi].rearrange("p t (c i) -> p c t i", i=LINE)
            engine.tensor_tensor(out=dst, in0=own, in1=share.rearrange("p t (c i) -> p c t i", i=LINE), op=ALU.add)

        whole = [(0, N)]

        offs_t = load_list("offs_t", offs)
        xw = load_words("xw", x_words, T_LEFT)
        xs = load_scales_repeated("xs", x_scales, T_LEFT)
        w1_raw = [load_weight_half("w1_raw%d" % h, w1, h) for h in range(2)]
        u1 = load_unit("u1", unit)
        rgt_t = load_list("rgt_t", rgt)
        es = load_scales_cleared("es", e_scales, T_RIGHT)
        ew = load_words("ew", e_words, T_RIGHT)
        ln_t = load_list("ln_t", ln)
        w2_raw = [load_weight_half("w2_raw%d" % h, w2, h) for h in range(2)]
        u2 = load_unit("u2", unit2)
        rn_t = load_list("rn_t", rn)
        dsp_t = load_list("dsp_t", dsp)

        xq = (pick("xq_w", xw, offs_t, U32, "xq_w"), pick("xq_s", xs, offs_t, U8, "xq_s"))
        w1b = sb.tile([P, PACK, P, PACK], BF16, name="w1b", tag="w1b", align_bytes=64)
        round_weight(nc.scalar.copy, w1b, w1_raw[0], 0, 0, M_HALF)
        round_weight(nc.vector.tensor_copy, w1b, w1_raw[1], 1, 0, M_VECTOR)
        round_weight(nc.scalar.copy, w1b, w1_raw[1], 1, M_VECTOR, M_HALF)
        w1q = mx_tiles("w1q", "w1q")
        y_pad = sb.tile([P, (PACK + 1) * N], F32, name="y_pad")
        nc.vector.memset(y_pad[:, PACK * N :], 0.0)
        y = y_pad[:, : PACK * N].rearrange("p (t n) -> p t n", t=PACK)
        yl = sb.tile([P, PACK, EARLY], F32, name="yl")
        for t in reversed(range(PACK)):
            quantize_weight_plane(w1q, w1b, t)
        for t in reversed(range(PACK)):
            acc = product(t, w1q, t, xq, whole)
            if t == 1:
                nc.vector.tensor_scalar(out=y[:, t, :], in0=acc[:], scalar1=u1[:, t : t + 1], scalar2=None, op0=ALU.mult)
            else:
                nc.scalar.activation(y[:, t, :], acc[:], COPY, scale=u1[:, t : t + 1])
        for t in reversed(range(PACK)):
            fetch(yl[:, t, :], y_pad[:, t * N : (t + 2) * N], ln_t, 0, EARLY, NEIGHBOUR)

        eq = (pick("eq_w", ew, rgt_t, U32, "xq_w"), pick("eq_s", es, rgt_t, U8, "w1b"))
        w2b = sb.tile([P, PACK, P, PACK], BF16, name="w2b", tag="ew", align_bytes=64)
        for h in range(2):
            round_weight(nc.vector.tensor_copy, w2b, w2_raw[h], h, 0, M_HALF)
        w2q = mx_tiles("w2q", "w2q")
        ye = sb.tile([P, PACK, N], F32, name="ye")
        for t in range(PACK):
            quantize_weight_plane(w2q, w2b, t)
        for t in range(PACK):
            acc = product(PACK + t, w2q, t, eq, whole)
            nc.vector.tensor_scalar(out=ye[:, t, :], in0=acc[:], scalar1=u2[:, t : t + 1], scalar2=None, op0=ALU.mult)
        hq = mx_tiles("hq", "xq_w")
        h2q = mx_tiles("h2q", "h2q")
        yr_halves = [sb.tile([P, PACK, HALF], F32, name="yr", tag=tag, align_bytes=64) for tag in ("yr0", "u2")]
        for k, (lo, hi) in enumerate(PIECES):
            yr = yr_halves[lo // HALF][:, :, lo % HALF : lo % HALF + hi - lo]
            for t in range(PACK):
                fetch(yr[:, t, :], ye[:, t, :], rn_t, lo, hi, NEIGHBOUR)
            hid2 = sb.tile([P, PACK * (hi - lo)], BF16, name="hid2", tag="hid2_%d" % k, align_bytes=64)
            combine(nc.vector, hid2[:], ye, yr, lo, hi)
            quantize(h2q, hid2[:], lo, hi)

        yl_late = sb.tile([P, PACK, P], F32, name="yl_late", tag="yr0", align_bytes=64)
        for t in range(PACK):
            fetch(yl_late[:, t, :], y[:, t, :], ln_t, EARLY, N, NEIGHBOUR)

        hid_0 = sb.tile([P, PACK * P], BF16, name="hid_0", align_bytes=64)
        hid_1 = sb.tile([P, PACK * P], BF16, name="hid_1", tag="w1b", align_bytes=64)
        hid_23 = sb.tile([P, 2 * PACK * P], BF16, name="hid_23", tag="hid2_2", align_bytes=64)
        hid = [hid_0[:], hid_1[:], hid_23[:, : PACK * P], hid_23[:, PACK * P :]]
        last = PACK - 1

        def add_chunk(m):
            share = yl_late[:] if m == last else yl[:, :, m * P : (m + 1) * P]
            combine(nc.gpsimd if m in (0, last) else nc.vector, hid[m], y, share, m * P, (m + 1) * P)

        def quantize_chunk(m):
            quantize(hq, hid[m], m * P, (m + 1) * P)

        add_chunk(0)
        add_chunk(1)
        quantize_chunk(0)
        quantize_chunk(1)
        add_chunk(2)
        quantize_chunk(2)

        scores = []
        for m in range(PACK):
            if m == last:
                add_chunk(m)
                quantize_chunk(m)
            sc = sb.tile([P, N + SPARE], F32, name="sc%d" % m)
            nc.vector.memset(sc[:, N:], 0.0)
            if m == 0:
                split = PIECES[-1][0]
                parts = [
                    (product(0, hq, m, h2q, PIECES[:-1]), slice(0, split)),
                    (product(PACK, hq, m, h2q, PIECES[-1:]), slice(split, N)),
                ]
                for acc, cols in parts:
                    nc.scalar.copy(out=sc[:, cols], in_=acc[:, cols])
            else:
                acc = product(m, hq, m, h2q, whole)
                nc.vector.tensor_copy(out=sc[:, :N], in_=acc[:])
                parts = [(acc, slice(0, HALF)), (acc, slice(HALF, N))] if m == last else [(acc, slice(0, N))]
            shifted = sb.tile([P, N], F32, name="shifted%d" % m)
            for lo, hi in [(0, HALF), (HALF, N)] if m == last else whole:
                fetch(shifted[:, lo:hi], sc[:], dsp_t, lo, hi, DISPARITY)
            scores.append((parts, shifted))

        for m, (parts, shifted) in enumerate(scores):
            rows = slice(m * P, (m + 1) * P)
            res = sb.tile([P, N], F32, name="res", tag=("hid2_2", "h2q", "xq_w", "res3")[m], align_bytes=64)
            for acc, cols in parts:
                nc.vector.tensor_tensor(out=res[:, cols], in0=shifted[:, cols], in1=acc[:, cols], op=ALU.max)
                if m == last:
                    nc.sync.dma_start(out=out[rows, cols], in_=res[:, cols])
            if m != last:
                nc.sync.dma_start(out=out[rows, :], in_=res[:])
